import numpy as np, ml_dtypes
CORES = [83,219,339,475,86,222,342,478]
N = 8
KB, QP = 2, 128
def setup_inputs(rng):
    return {"q": rng.standard_normal((N, 128, QP), dtype=np.float32).astype(ml_dtypes.bfloat16), "k": rng.standard_normal((N, 128, KB * 128), dtype=np.float32).astype(ml_dtypes.bfloat16), "v": rng.standard_normal((N, 128, KB * 128), dtype=np.float32).astype(ml_dtypes.bfloat16)}
def reference(q, k, v):
    Q, K, V = q.astype(np.float64), k.astype(np.float64), v.astype(np.float64)
    y = np.zeros((N, 128, QP))
    for r in range(N):
        for j in range(N):
            for b in range(KB):
                S = np.maximum(K[j][:, 128 * b:128 * b + 128].T @ Q[r], 0.0)
                y[r] += V[j][:, 128 * b:128 * b + 128].T @ S
    return {"y": y.astype(ml_dtypes.bfloat16 if q.dtype != np.float64 else np.float64)}

@@ -1,0 +1,134 @@
+from concourse.bass import DstId, RemoteDMATransfer
+from concourse.mybir import AluOpType
+
+_BF, _F32 = "bfloat16", "float32"
+SCRATCH = {
+    "lq": ("sbuf", [128, 256], _BF),
+    "xq": ("sbuf", [128, 256], _BF),
+    "kv": ("sbuf", [128, 512], _BF),
+    "rkv": ("sbuf", [128, 512], _BF),
+    "zero": ("sbuf", [128, 512], _F32),
+    "rLa": ("sbuf", [128, 512], _BF),
+    "rXa": ("sbuf", [128, 512], _BF),
+    "rXb0": ("sbuf", [128, 256], _BF),
+    "rXb1": ("sbuf", [128, 256], _BF),
+    "rLb": ("sbuf", [128, 512], _BF),
+    "oX": ("sbuf", [128, 256], _BF),
+    "oP": ("sbuf", [128, 128], _BF),
+    "inX": ("sbuf", [128, 256], _BF),
+    "inP": ("sbuf", [128, 128], _BF),
+    "yo": ("sbuf", [128, 128], _BF),
+    "p0": ("psum", [128, 512], _F32), "p1": ("psum", [128, 512], _F32), "p2": ("psum", [128, 512], _F32),
+    "p3": ("psum", [128, 512], _F32), "p4": ("psum", [128, 512], _F32), "p5": ("psum", [128, 512], _F32),
+    "p6": ("psum", [128, 512], _F32), "p7": ("psum", [128, 512], _F32),
+}
+SEMAPHORES = ["ld_q", "ld_kv", "stored", "sent", "pq", "xq", "rkv", "ox0", "ox1", "op", "z",
+              "sLa", "sXa", "sXb0", "sXb1", "sLb", "rLa", "rXa", "rXb0", "rXb1", "rLb",
+              "oL", "oX", "cX", "cP", "a1", "a2", "yr"]
+
+
+def rank_program(g, core, T, topo):
+    r = T.rank_of(core)
+    if r is None:
+        return
+    c, s = r % 4, r // 4
+    sem, pe, ve = T.sem, g.tensor, g.vector
+
+    def at(cc, ss):
+        return T.cores[cc + 4 * ss]
+
+    partner, rack_nb, far = at(c, 1 - s), at(c ^ 1, s), (at(3 - c, 0), at(3 - c, 1))
+    mine = slice(128 * s, 128 * s + 128)
+
+    def xfer(dst_core, mask, rsem, src, dst):
+        rid, pid = topo.addr(dst_core, core)
+        return RemoteDMATransfer(dst_ids=[DstId(rid=rid, pnc=pid)], dma_engine_mask=mask, remote_sem=rsem,
+                                 src=src, dst=dst)
+
+    g.sync.dma_start(T.lq[:, 0:128], T.q[:, :]).then_inc(sem.ld_q, 16)
+    g.scalar.dma_start(T.kv[:, 0:256], T.k[:, :]).then_inc(sem.ld_kv, 16)
+    g.sync.dma_start(T.kv[:, 256:512], T.v[:, :]).then_inc(sem.ld_kv, 16)
+
+    g.wait_ge(sem.ld_q, 16)
+    g.remote_dma_fused([
+        xfer(far[0], 0x000F, sem.xq, T.lq[:, 0:128], T.xq[:, mine]),
+        xfer(far[1], 0x00F0, sem.xq, T.lq[:, 0:128], T.xq[:, mine]),
+        xfer(partner, 0xFF00, sem.pq, T.lq[:, 0:128], T.lq[:, 128:256]),
+    ], local_sem=sem.sent)
+    g.wait_ge(sem.ld_kv, 32)
+    g.remote_dma_fused([xfer(rack_nb, 0x00FF, sem.rkv, T.kv[:], T.rkv[:])], local_sem=sem.sent)
+    g.wait_ge(sem.cX, 1)
+    g.remote_dma_fused([
+        xfer(far[0], 0x000F, sem["ox%d" % s], T.oX[:, 0:128], T.inX[:, mine]),
+        xfer(far[1], 0x00F0, sem["ox%d" % s], T.oX[:, 128:256], T.inX[:, mine]),
+    ], local_sem=sem.sent)
+    g.wait_ge(sem.cP, 1)
+    g.remote_dma_fused([xfer(partner, 0xFF00, sem.op, T.oP[:], T.inP[:])], local_sem=sem.sent)
+    g.wait_ge(sem.sent, 16 + 8 + 8 + 8)
+
+    def kb(buf, b):
+        return buf[:, 128 * b:128 * b + 128]
+
+    def vb(buf, b):
+        return buf[:, 256 + 128 * b:256 + 128 * b + 128]
+
+    def mm(out, lhsT, rhs, start, stop, done):
+        pe.matmul(out, lhsT, rhs, start, stop).then_inc(done, 1)
+
+    def half(buf, b):
+        return buf[:, 256 * b:256 * b + 256]
+
+    pe.wait_ge(sem.ld_q, 16)
+    pe.wait_ge(sem.ld_kv, 32)
+    pe.wait_ge(sem.pq, 8)
+    for b in (0, 1):
+        mm(half(T.p0, b), kb(T.kv, b), T.lq[:], True, True, sem.sLa)
+    pe.wait_ge(sem.xq, 8)
+    for b in (0, 1):
+        mm(half(T.p1, b), kb(T.kv, b), T.xq[:], True, True, sem.sXa)
+    pe.wait_ge(sem.rLa, 1)
+    for b in (0, 1):
+        mm(T.p6[:, 0:256], vb(T.kv, b), half(T.rLa, b), b == 0, False, sem.oL)
+    pe.wait_ge(sem.rXa, 1)
+    for b in (0, 1):
+        mm(T.p7[:, 0:256], vb(T.kv, b), half(T.rXa, b), b == 0, False, sem.oX)
+    pe.wait_ge(sem.rkv, 8)
+    mm(T.p2[:, 0:256], kb(T.rkv, 0), T.xq[:], True, True, sem.sXb0)
+    mm(T.p3[:, 0:256], kb(T.rkv, 1), T.xq[:], True, True, sem.sXb1)
+    pe.wait_ge(sem.rXb0, 1)
+    mm(T.p7[:, 0:256], vb(T.rkv, 0), T.rXb0[:], False, False, sem.oX)
+    pe.wait_ge(sem.rXb1, 1)
+    mm(T.p7[:, 0:256], vb(T.rkv, 1), T.rXb1[:], False, True, sem.oX)
+    for b in (0, 1):
+        mm(half(T.p4, b), kb(T.rkv, b), T.lq[:], True, True, sem.sLb)
+    pe.wait_ge(sem.rLb, 1)
+    for b in (0, 1):
+        mm(T.p6[:, 0:256], vb(T.rkv, b), half(T.rLb, b), False, b == 1, sem.oL)
+
+    def relu(dst, src, n, ready, count, done):
+        ve.wait_ge(ready, count)
+        ve.tensor_tensor(dst, src, T.zero[:, 0:n], AluOpType.max).then_inc(done, 1)
+
+    ve.memset(T.zero[:], 0.0).then_inc(sem.z, 1)
+    ve.wait_ge(sem.z, 1)
+    relu(T.rLa[:], T.p0[:], 512, sem.sLa, 2, sem.rLa)
+    relu(T.rXa[:], T.p1[:], 512, sem.sXa, 2, sem.rXa)
+    relu(T.rXb0[:], T.p2[:, 0:256], 256, sem.sXb0, 1, sem.rXb0)
+    relu(T.rXb1[:], T.p3[:, 0:256], 256, sem.sXb1, 1, sem.rXb1)
+    ve.wait_ge(sem.oX, 4)
+    ve.tensor_copy(T.oX[:], T.p7[:, 0:256]).then_inc(sem.cX, 1)
+    relu(T.rLb[:], T.p4[:], 512, sem.sLb, 2, sem.rLb)
+    ve.wait_ge(sem.oL, 4)
+    ve.tensor_copy(T.oP[:], T.p6[:, 128:256]).then_inc(sem.cP, 1)
+    ve.wait_ge(sem.op, 8)
+    ve.tensor_tensor(T.p5[:, 0:128], T.p6[:, 0:128], T.inP[:], AluOpType.add).then_inc(sem.a1, 1)
+    ve.wait_ge(sem.a1, 1)
+    ve.wait_ge(sem.ox0, 4)
+    ve.tensor_tensor(T.p5[:, 128:256], T.p5[:, 0:128], T.inX[:, 0:128], AluOpType.add).then_inc(sem.a2, 1)
+    ve.wait_ge(sem.a2, 1)
+    ve.wait_ge(sem.ox1, 4)
+    ve.tensor_tensor(T.yo[:], T.p5[:, 128:256], T.inX[:, 128:256], AluOpType.add).then_inc(sem.yr, 1)
+
+    g.sync.wait_ge(sem.yr, 1)
+    g.sync.dma_start(T.y[:, :], T.yo[:]).then_inc(sem.stored, 16)
+    g.sync.wait_ge(sem.stored, 16)

@@ -51,12 +51,12 @@ def rank_program(g, core, T, topo):
 
     g.wait_ge(sem.ld_q, 16)
     g.remote_dma_fused([
-        xfer(far[0], 0x000F, sem.xq, T.lq[:, 0:128], T.xq[:, mine]),
-        xfer(far[1], 0x00F0, sem.xq, T.lq[:, 0:128], T.xq[:, mine]),
-        xfer(partner, 0xFF00, sem.pq, T.lq[:, 0:128], T.lq[:, 128:256]),
+        xfer(far[0], 0x0003, sem.xq, T.lq[:, 0:128], T.xq[:, mine]),
+        xfer(far[1], 0x000C, sem.xq, T.lq[:, 0:128], T.xq[:, mine]),
+        xfer(partner, 0x0F00, sem.pq, T.lq[:, 0:128], T.lq[:, 128:256]),
     ], local_sem=sem.sent)
     g.wait_ge(sem.ld_kv, 32)
-    g.remote_dma_fused([xfer(rack_nb, 0x00FF, sem.rkv, T.kv[:], T.rkv[:])], local_sem=sem.sent)
+    g.remote_dma_fused([xfer(rack_nb, 0x00F0, sem.rkv, T.kv[:], T.rkv[:])], local_sem=sem.sent)
     g.wait_ge(sem.cX, 1)
     g.remote_dma_fused([
         xfer(far[0], 0x000F, sem["ox%d" % s], T.oX[:, 0:128], T.inX[:, mine]),
@@ -64,7 +64,7 @@ def rank_program(g, core, T, topo):
     ], local_sem=sem.sent)
     g.wait_ge(sem.cP, 1)
     g.remote_dma_fused([xfer(partner, 0xFF00, sem.op, T.oP[:], T.inP[:])], local_sem=sem.sent)
-    g.wait_ge(sem.sent, 16 + 8 + 8 + 8)
+    g.wait_ge(sem.sent, 8 + 4 + 8 + 8)
 
     def kb(buf, b):
         return buf[:, 128 * b:128 * b + 128]
@@ -80,10 +80,10 @@ def rank_program(g, core, T, topo):
 
     pe.wait_ge(sem.ld_q, 16)
     pe.wait_ge(sem.ld_kv, 32)
-    pe.wait_ge(sem.pq, 8)
+    pe.wait_ge(sem.pq, 4)
     for b in (0, 1):
         mm(half(T.p0, b), kb(T.kv, b), T.lq[:], True, True, sem.sLa)
-    pe.wait_ge(sem.xq, 8)
+    pe.wait_ge(sem.xq, 4)
     for b in (0, 1):
         mm(half(T.p1, b), kb(T.kv, b), T.xq[:], True, True, sem.sXa)
     pe.wait_ge(sem.rLa, 1)
@@ -92,7 +92,7 @@ def rank_program(g, core, T, topo):
     pe.wait_ge(sem.rXa, 1)
     for b in (0, 1):
         mm(T.p7[:, 0:256], vb(T.kv, b), half(T.rXa, b), b == 0, False, sem.oX)
-    pe.wait_ge(sem.rkv, 8)
+    pe.wait_ge(sem.rkv, 4)
     mm(T.p2[:, 0:256], kb(T.rkv, 0), T.xq[:], True, True, sem.sXb0)
     mm(T.p3[:, 0:256], kb(T.rkv, 1), T.xq[:], True, True, sem.sXb1)
     pe.wait_ge(sem.rXb0, 1)

@@ -9,9 +9,10 @@ SCRATCH = {
     "rkv": ("sbuf", [128, 512], _BF),
     "zero": ("sbuf", [128, 512], _F32),
     "rLa": ("sbuf", [128, 512], _BF),
-    "rXa": ("sbuf", [128, 512], _BF),
-    "rXb0": ("sbuf", [128, 256], _BF),
-    "rXb1": ("sbuf", [128, 256], _BF),
+    "rX0": ("sbuf", [128, 256], _BF),
+    "rX1": ("sbuf", [128, 256], _BF),
+    "rX2": ("sbuf", [128, 256], _BF),
+    "rX3": ("sbuf", [128, 256], _BF),
     "rLb": ("sbuf", [128, 512], _BF),
     "oX": ("sbuf", [128, 256], _BF),
     "oP": ("sbuf", [128, 128], _BF),
@@ -23,7 +24,7 @@ SCRATCH = {
     "p6": ("psum", [128, 512], _F32), "p7": ("psum", [128, 512], _F32),
 }
 SEMAPHORES = ["ld_q", "ld_kv", "stored", "sent", "pq", "xq", "rkv", "ox0", "ox1", "op", "z",
-              "sLa", "sXa", "sXb0", "sXb1", "sLb", "rLa", "rXa", "rXb0", "rXb1", "rLb",
+              "sLa", "sX0", "sX1", "sX2", "sX3", "sLb", "rLa", "rX0", "rX1", "rX2", "rX3", "rLb",
               "oL", "oX", "cX", "cP", "a1", "a2", "yr"]
 
 
@@ -78,29 +79,35 @@ def rank_program(g, core, T, topo):
     def half(buf, b):
         return buf[:, 256 * b:256 * b + 256]
 
+    xs = [(T.kv, 0, T.p1, T.rX0), (T.kv, 1, T.p5, T.rX1), (T.rkv, 0, T.p2, T.rX2), (T.rkv, 1, T.p3, T.rX3)]
+
+    def x_scores(i):
+        buf, b, bank, _ = xs[i]
+        mm(bank[:, 0:256], kb(buf, b), T.xq[:], True, True, sem["sX%d" % i])
+
+    def x_values(i):
+        buf, b, _, relued = xs[i]
+        pe.wait_ge(sem["rX%d" % i], 1)
+        mm(T.p7[:, 0:256], vb(buf, b), relued[:], i == 0, i == 3, sem.oX)
+
     pe.wait_ge(sem.ld_q, 16)
     pe.wait_ge(sem.ld_kv, 32)
     pe.wait_ge(sem.pq, 4)
     for b in (0, 1):
         mm(half(T.p0, b), kb(T.kv, b), T.lq[:], True, True, sem.sLa)
     pe.wait_ge(sem.xq, 4)
+    x_scores(0)
+    x_scores(1)
+    pe.wait_ge(sem.rkv, 4)
+    x_scores(2)
+    x_scores(3)
+    for i in range(4):
+        x_values(i)
     for b in (0, 1):
-        mm(half(T.p1, b), kb(T.kv, b), T.xq[:], True, True, sem.sXa)
+        mm(half(T.p4, b), kb(T.rkv, b), T.lq[:], True, True, sem.sLb)
     pe.wait_ge(sem.rLa, 1)
     for b in (0, 1):
         mm(T.p6[:, 0:256], vb(T.kv, b), half(T.rLa, b), b == 0, False, sem.oL)
-    pe.wait_ge(sem.rXa, 1)
-    for b in (0, 1):
-        mm(T.p7[:, 0:256], vb(T.kv, b), half(T.rXa, b), b == 0, False, sem.oX)
-    pe.wait_ge(sem.rkv, 4)
-    mm(T.p2[:, 0:256], kb(T.rkv, 0), T.xq[:], True, True, sem.sXb0)
-    mm(T.p3[:, 0:256], kb(T.rkv, 1), T.xq[:], True, True, sem.sXb1)
-    pe.wait_ge(sem.rXb0, 1)
-    mm(T.p7[:, 0:256], vb(T.rkv, 0), T.rXb0[:], False, False, sem.oX)
-    pe.wait_ge(sem.rXb1, 1)
-    mm(T.p7[:, 0:256], vb(T.rkv, 1), T.rXb1[:], False, True, sem.oX)
-    for b in (0, 1):
-        mm(half(T.p4, b), kb(T.rkv, b), T.lq[:], True, True, sem.sLb)
     pe.wait_ge(sem.rLb, 1)
     for b in (0, 1):
         mm(T.p6[:, 0:256], vb(T.rkv, b), half(T.rLb, b), False, b == 1, sem.oL)
@@ -112,22 +119,21 @@ def rank_program(g, core, T, topo):
     ve.memset(T.zero[:], 0.0).then_inc(sem.z, 1)
     ve.wait_ge(sem.z, 1)
     relu(T.rLa[:], T.p0[:], 512, sem.sLa, 2, sem.rLa)
-    relu(T.rXa[:], T.p1[:], 512, sem.sXa, 2, sem.rXa)
-    relu(T.rXb0[:], T.p2[:, 0:256], 256, sem.sXb0, 1, sem.rXb0)
-    relu(T.rXb1[:], T.p3[:, 0:256], 256, sem.sXb1, 1, sem.rXb1)
+    for i in range(4):
+        relu(xs[i][3][:], xs[i][2][:, 0:256], 256, sem["sX%d" % i], 1, sem["rX%d" % i])
     ve.wait_ge(sem.oX, 4)
     ve.tensor_copy(T.oX[:], T.p7[:, 0:256]).then_inc(sem.cX, 1)
     relu(T.rLb[:], T.p4[:], 512, sem.sLb, 2, sem.rLb)
     ve.wait_ge(sem.oL, 4)
     ve.tensor_copy(T.oP[:], T.p6[:, 128:256]).then_inc(sem.cP, 1)
     ve.wait_ge(sem.op, 8)
-    ve.tensor_tensor(T.p5[:, 0:128], T.p6[:, 0:128], T.inP[:], AluOpType.add).then_inc(sem.a1, 1)
+    ve.tensor_tensor(T.p1[:, 0:128], T.p6[:, 0:128], T.inP[:], AluOpType.add).then_inc(sem.a1, 1)
     ve.wait_ge(sem.a1, 1)
     ve.wait_ge(sem.ox0, 4)
-    ve.tensor_tensor(T.p5[:, 128:256], T.p5[:, 0:128], T.inX[:, 0:128], AluOpType.add).then_inc(sem.a2, 1)
+    ve.tensor_tensor(T.p1[:, 128:256], T.p1[:, 0:128], T.inX[:, 0:128], AluOpType.add).then_inc(sem.a2, 1)
     ve.wait_ge(sem.a2, 1)
     ve.wait_ge(sem.ox1, 4)
-    ve.tensor_tensor(T.yo[:], T.p5[:, 128:256], T.inX[:, 128:256], AluOpType.add).then_inc(sem.yr, 1)
+    ve.tensor_tensor(T.yo[:], T.p1[:, 128:256], T.inX[:, 128:256], AluOpType.add).then_inc(sem.yr, 1)
 
     g.sync.wait_ge(sem.yr, 1)
     g.sync.dma_start(T.y[:, :], T.yo[:]).then_inc(sem.stored, 16)

from concourse.bass import DstId, RemoteDMATransfer
from concourse.mybir import AluOpType

_BF, _F32 = "bfloat16", "float32"
SCRATCH = {
    "lq": ("sbuf", [128, 256], _BF),
    "xq": ("sbuf", [128, 256], _BF),
    "kv": ("sbuf", [128, 512], _BF),
    "rkv": ("sbuf", [128, 512], _BF),
    "zero": ("sbuf", [128, 512], _F32),
    "rLa": ("sbuf", [128, 512], _BF),
    "rX0": ("sbuf", [128, 256], _BF),
    "rX1": ("sbuf", [128, 256], _BF),
    "rX2": ("sbuf", [128, 256], _BF),
    "rX3": ("sbuf", [128, 256], _BF),
    "rLb": ("sbuf", [128, 512], _BF),
    "oX": ("sbuf", [128, 256], _BF),
    "oP": ("sbuf", [128, 128], _BF),
    "inX": ("sbuf", [128, 256], _BF),
    "inP": ("sbuf", [128, 128], _BF),
    "yo": ("sbuf", [128, 128], _BF),
    "p0": ("psum", [128, 512], _F32), "p1": ("psum", [128, 512], _F32), "p2": ("psum", [128, 512], _F32),
    "p3": ("psum", [128, 512], _F32), "p4": ("psum", [128, 512], _F32), "p5": ("psum", [128, 512], _F32),
    "p6": ("psum", [128, 512], _F32), "p7": ("psum", [128, 512], _F32),
}
SEMAPHORES = ["ld_q", "ld_kv", "stored", "sent", "pq", "xq", "rkv", "ox0", "ox1", "op", "z",
              "sLa", "sX0", "sX1", "sX2", "sX3", "sLb", "rLa", "rX0", "rX1", "rX2", "rX3", "rLb",
              "oL", "oX", "cX", "cP", "a1", "a2", "yr"]


def rank_program(g, core, T, topo):
    r = T.rank_of(core)
    if r is None:
        return
    c, s = r % 4, r // 4
    sem, pe, ve = T.sem, g.tensor, g.vector

    def at(cc, ss):
        return T.cores[cc + 4 * ss]

    partner, rack_nb, far = at(c, 1 - s), at(c ^ 1, s), (at(3 - c, 0), at(3 - c, 1))
    mine = slice(128 * s, 128 * s + 128)

    def xfer(dst_core, mask, rsem, src, dst):
        rid, pid = topo.addr(dst_core, core)
        return RemoteDMATransfer(dst_ids=[DstId(rid=rid, pnc=pid)], dma_engine_mask=mask, remote_sem=rsem,
                                 src=src, dst=dst)

    g.sync.dma_start(T.lq[:, 0:128], T.q[:, :]).then_inc(sem.ld_q, 16)
    g.scalar.dma_start(T.kv[:, 0:256], T.k[:, :]).then_inc(sem.ld_kv, 16)
    g.sync.dma_start(T.kv[:, 256:512], T.v[:, :]).then_inc(sem.ld_kv, 16)

    g.wait_ge(sem.ld_q, 16)
    g.remote_dma_fused([
        xfer(far[0], 0x0003, sem.xq, T.lq[:, 0:128], T.xq[:, mine]),
        xfer(far[1], 0x000C, sem.xq, T.lq[:, 0:128], T.xq[:, mine]),
        xfer(partner, 0x0F00, sem.pq, T.lq[:, 0:128], T.lq[:, 128:256]),
    ], local_sem=sem.sent)
    g.wait_ge(sem.ld_kv, 32)
    g.remote_dma_fused([xfer(rack_nb, 0x00F0, sem.rkv, T.kv[:], T.rkv[:])], local_sem=sem.sent)
    g.wait_ge(sem.cX, 1)
    g.remote_dma_fused([
        xfer(far[0], 0x000F, sem["ox%d" % s], T.oX[:, 0:128], T.inX[:, mine]),
        xfer(far[1], 0x00F0, sem["ox%d" % s], T.oX[:, 128:256], T.inX[:, mine]),
    ], local_sem=sem.sent)
    g.wait_ge(sem.cP, 1)
    g.remote_dma_fused([xfer(partner, 0xFF00, sem.op, T.oP[:], T.inP[:])], local_sem=sem.sent)
    g.wait_ge(sem.sent, 8 + 4 + 8 + 8)

    def kb(buf, b):
        return buf[:, 128 * b:128 * b + 128]

    def vb(buf, b):
        return buf[:, 256 + 128 * b:256 + 128 * b + 128]

    def mm(out, lhsT, rhs, start, stop, done):
        pe.matmul(out, lhsT, rhs, start, stop).then_inc(done, 1)

    def half(buf, b):
        return buf[:, 256 * b:256 * b + 256]

    xs = [(T.kv, 0, T.p1, T.rX0), (T.kv, 1, T.p5, T.rX1), (T.rkv, 0, T.p2, T.rX2), (T.rkv, 1, T.p3, T.rX3)]

    def x_scores(i):
        buf, b, bank, _ = xs[i]
        mm(bank[:, 0:256], kb(buf, b), T.xq[:], True, True, sem["sX%d" % i])

    def x_values(i):
        buf, b, _, relued = xs[i]
        pe.wait_ge(sem["rX%d" % i], 1)
        mm(T.p7[:, 0:256], vb(buf, b), relued[:], i == 0, i == 3, sem.oX)

    pe.wait_ge(sem.ld_q, 16)
    pe.wait_ge(sem.ld_kv, 32)
    pe.wait_ge(sem.pq, 4)
    for b in (0, 1):
        mm(half(T.p0, b), kb(T.kv, b), T.lq[:], True, True, sem.sLa)
    pe.wait_ge(sem.xq, 4)
    x_scores(0)
    x_scores(1)
    pe.wait_ge(sem.rkv, 4)
    x_scores(2)
    x_scores(3)
    for i in range(4):
        x_values(i)
    for b in (0, 1):
        mm(half(T.p4, b), kb(T.rkv, b), T.lq[:], True, True, sem.sLb)
    pe.wait_ge(sem.rLa, 1)
    for b in (0, 1):
        mm(T.p6[:, 0:256], vb(T.kv, b), half(T.rLa, b), b == 0, False, sem.oL)
    pe.wait_ge(sem.rLb, 1)
    for b in (0, 1):
        mm(T.p6[:, 0:256], vb(T.rkv, b), half(T.rLb, b), False, b == 1, sem.oL)

    def relu(dst, src, n, ready, count, done):
        ve.wait_ge(ready, count)
        ve.tensor_tensor(dst, src, T.zero[:, 0:n], AluOpType.max).then_inc(done, 1)

    ve.memset(T.zero[:], 0.0).then_inc(sem.z, 1)
    ve.wait_ge(sem.z, 1)
    relu(T.rLa[:], T.p0[:], 512, sem.sLa, 2, sem.rLa)
    for i in range(4):
        relu(xs[i][3][:], xs[i][2][:, 0:256], 256, sem["sX%d" % i], 1, sem["rX%d" % i])
    ve.wait_ge(sem.oX, 4)
    ve.tensor_copy(T.oX[:], T.p7[:, 0:256]).then_inc(sem.cX, 1)
    relu(T.rLb[:], T.p4[:], 512, sem.sLb, 2, sem.rLb)
    ve.wait_ge(sem.oL, 4)
    ve.tensor_copy(T.oP[:], T.p6[:, 128:256]).then_inc(sem.cP, 1)
    ve.wait_ge(sem.op, 8)
    ve.tensor_tensor(T.p1[:, 0:128], T.p6[:, 0:128], T.inP[:], AluOpType.add).then_inc(sem.a1, 1)
    ve.wait_ge(sem.a1, 1)
    ve.wait_ge(sem.ox0, 4)
    ve.tensor_tensor(T.p1[:, 128:256], T.p1[:, 0:128], T.inX[:, 0:128], AluOpType.add).then_inc(sem.a2, 1)
    ve.wait_ge(sem.a2, 1)
    ve.wait_ge(sem.ox1, 4)
    ve.tensor_tensor(T.yo[:], T.p1[:, 128:256], T.inX[:, 128:256], AluOpType.add).then_inc(sem.yr, 1)

    g.sync.wait_ge(sem.yr, 1)
    g.sync.dma_start(T.y[:, :], T.yo[:]).then_inc(sem.stored, 16)
    g.sync.wait_ge(sem.stored, 16)
